import numpy as np
import ml_dtypes


def mxq(x, axis, fmt="e4m3"):
    dtype, down = {"e4m3": (ml_dtypes.float8_e4m3fn, 7), "e5m2": (ml_dtypes.float8_e5m2, 14)}[fmt]
    v = np.moveaxis(np.asarray(x, np.float32).astype(ml_dtypes.bfloat16).astype(np.float64), axis, -1)
    blocks = v.reshape(v.shape[:-1] + (-1, 32))
    amax = np.abs(blocks).max(-1, keepdims=True)
    byte = np.maximum(np.where(amax > 0, np.frexp(amax)[1] - 1 + 127, 0) - down, 1)
    scale = np.exp2(byte - 127.0)
    codes = (blocks / scale).astype(np.float32).astype(dtype).astype(np.float64)
    return np.moveaxis((codes * scale).reshape(v.shape), -1, axis)


WIDE = False


def mx_kscale(k):
    if not WIDE:
        return np.ones(k)
    levels = np.array([10, -10, 5, -5, 0])
    if k % 512:
        return np.exp2(np.random.permutation(np.resize(levels, k // 32))).repeat(32)
    a = np.empty((k // 512, 16))
    for p in range(k // 512):
        a[p, :8] = np.random.permutation(np.resize(levels, 8))
        for g in range(8):
            far = levels[np.abs(levels - a[p, g]) >= 10]
            a[p, g + 8] = far[np.random.randint(len(far))]
    return np.exp2(a.ravel()).repeat(32)


def f64(x):
    return np.asarray(x).astype(np.float64)


def striped(idx):
    return np.tile(idx.reshape(-1, 16).T, (8, 1)).astype(np.uint16)


def unstriped(offs):
    return offs[:16].T.reshape(-1).astype(np.int64)


def striped8(idx):
    return np.concatenate([x.reshape(-1, 16).T for x in idx]).astype(np.uint16)


def runs(offs, k):
    lists = np.stack([offs[16 * r : 16 * r + 16].T.reshape(-1) for r in range(8)]).astype(np.int64)
    return lists[np.arange(k) % 512 // 64]


def pack_weight(w):
    k, n = w.shape
    w = f64(np.asarray(w, np.float32).astype(ml_dtypes.bfloat16)).reshape(k // 32, 32, n)
    amax = np.abs(w).max(1)
    byte = np.clip(np.where(amax > 0, np.frexp(amax)[1] - 1 + 127 - 7, 1), 1, 254)
    scaled = (w * np.exp2(127.0 - byte)[:, None, :]).reshape(k, n).astype(np.float32)
    words = np.ascontiguousarray(scaled.reshape(k // 512, 128, 4, n).transpose(0, 1, 3, 2)).astype(ml_dtypes.float8_e4m3fn).view(np.uint8)
    return words, np.ascontiguousarray(byte.astype(np.uint8).reshape(k // 512, 16, n))


def unpack_weight(words, scales):
    g, p, n, _ = words.shape
    vals = np.ascontiguousarray(words).view(ml_dtypes.float8_e4m3fn).astype(np.float64) * np.repeat(np.exp2(scales.astype(np.float64) - 127.0), 8, axis=1)[..., None]
    return vals.transpose(0, 1, 3, 2).reshape(g * 512, n)

def planes(y):
    n, m = y.shape
    v = y.astype(np.float32).astype(ml_dtypes.bfloat16).astype(np.float64).reshape(n // 32, 32, m)
    top = np.abs(v).max(1)
    byte = np.clip(np.where(top > 0, np.frexp(top)[1] - 1 + 127 - 7, 1), 1, 254)
    codes = (v * np.exp2(127.0 - byte)[:, None, :]).reshape(n, m).astype(np.float32).astype(ml_dtypes.float8_e4m3fn).view(np.uint8)
    words = codes.reshape(n // 512, 128, 4, m).transpose(0, 1, 3, 2)
    return np.ascontiguousarray(words), np.ascontiguousarray(byte.astype(np.uint8).reshape(n // 512, 16, m))


K, T, S, G, H, W = 512, 1024, 256, 2048, 512, 128


def setup_inputs():
    n = np.random.standard_normal
    s = mx_kscale(K)[:, None]
    packed_xT = pack_weight(n((K, T)) * s)
    packed_dT = pack_weight(n((K, G)) / s)
    perm = np.random.permutation(S)
    perm2 = np.random.permutation(S)
    perm3 = np.random.permutation(S)
    return {
        "x_words": packed_xT[0],
        "x_scales": packed_xT[1],
        "d_words": packed_dT[0],
        "d_scales": packed_dT[1],
        "gs": (np.random.uniform(0.5, 1.5, (K, 1)) * s).astype(np.float32),
        "offs": striped8(np.random.randint(0, T, (8, S))),
        "k1": striped8(np.random.randint(0, G, (8, H))),
        "hz": striped8(np.random.randint(0, T, (8, S))),
        "k2": striped8(np.random.randint(0, G, (8, H))),
        "n1": striped(perm[:W]),
        "n2": striped(perm[W:]),
        "k3": striped8(np.random.randint(0, G, (8, H))),
        "k4": striped8(np.random.randint(0, G, (8, H))),
        "hy": striped8(np.random.randint(0, T, (8, S))),
        "n3": striped(perm2[:W]),
        "n4": striped(perm2[W:]),
        "n5": striped(perm3[:W]),
        "n6": striped(perm3[W:]),
        "n7": striped(np.random.permutation(S)),
    }


def reference(x_words, x_scales, d_words, d_scales, gs, offs, k1, hz, k2, n1, n2, k3, k4, hy, n3, n4, n5, n6, n7):
    d_k3 = unpack_weight(d_words, d_scales)[np.arange(K)[:, None], runs(k3, K)]
    d_k1 = unpack_weight(d_words, d_scales)[np.arange(K)[:, None], runs(k1, K)]
    xq = unpack_weight(x_words, x_scales)[np.arange(K)[:, None], runs(offs, K)]
    d_k2 = unpack_weight(d_words, d_scales)[np.arange(K)[:, None], runs(k2, K)]
    x_hz = unpack_weight(x_words, x_scales)[np.arange(K)[:, None], runs(hz, K)]
    h = 0.0625 * (d_k1.T @ xq + d_k2.T @ x_hz)
    pb = h[:, unstriped(n2)]
    pa = h[:, unstriped(n1)]
    rb = pb - (0.5 * pa)
    ra = np.sqrt((pa) ** 2 + (pb) ** 2 + 0.25)
    ua = np.zeros((H, S))
    ua[:, unstriped(n1)] = ra
    ub = ua.copy()
    ub[:, unstriped(n2)] = rb
    z = f64(gs) * ub
    d_k4 = unpack_weight(d_words, d_scales)[np.arange(K)[:, None], runs(k4, K)]
    x_hy = unpack_weight(x_words, x_scales)[np.arange(K)[:, None], runs(hy, K)]
    h2 = 0.0625 * ((d_k3.T @ mxq(z, 0, "e4m3") + d_k4.T @ x_hy))
    pa2 = h2[:, unstriped(n3)]
    pb2 = h2[:, unstriped(n4)]
    ra2 = pb2 - pa2
    ua2 = np.zeros((H, S))
    ua2[:, unstriped(n5)] = ra2
    ub2 = ua2.copy()
    ub2[:, unstriped(n6)] = pa2
    out_0 = np.maximum(ub2, h2[:, unstriped(n7)])
    return (out_0,) + planes(out_0)

@@ -1,0 +1,197 @@
+from contextlib import ExitStack
+
+import concourse.mybir as mybir
+
+F32 = mybir.dt.float32
+BF16 = mybir.dt.bfloat16
+I32 = mybir.dt.int32
+U32 = mybir.dt.uint32
+U16 = mybir.dt.uint16
+U8 = mybir.dt.uint8
+FP8X4 = mybir.dt.float8_e4m3fn_x4
+ALU = mybir.AluOpType
+ACT = mybir.ActivationFunctionType
+
+P = 128
+PACK = 4
+T = 1024
+G = 2048
+S = 256
+H = 512
+W = 128
+FLOPS = 4 * 2 * 512 * H * S
+
+
+def tile_picked_mhhzmhpolarcphw_none_po_kernel(
+    tc, x_words, x_scales, d_words, d_scales, gs, offs, k1, hz, k2, n1, n2, k3, k4, hy, n3, n4, n5, n6, n7,
+    out_0, out_1, out_2,
+):
+    nc = tc.nc
+    with ExitStack() as ctx:
+        keep = ctx.enter_context(tc.tile_pool(name="keep", bufs=1))
+        work = ctx.enter_context(tc.tile_pool(name="work", bufs=1))
+        psum = ctx.enter_context(tc.psum_pool(name="psum", bufs=1))
+
+        lists = {}
+
+        def load_list(name, src):
+            lists[name] = keep.tile([P, src.shape[1]], U16, name="list_" + name)
+            nc.sync.dma_start(lists[name][:], src)
+
+        def load_scales(name, src, width):
+            tile = keep.tile([P, width], U8, name=name, align_bytes=64)
+            rows = src[0].bitcast(I32)
+            nc.sync.dma_start(tile[:].bitcast(I32), rows.unsqueeze(1).to_broadcast([16, 8, width // 4]))
+            return tile
+
+        def load_words(name, src, width):
+            tile = keep.tile([P, width], U32, name=name, align_bytes=64)
+            nc.sync.dma_start(tile[:].bitcast(I32), src[0].rearrange("p c r -> p (c r)").bitcast(I32))
+            return tile
+
+        d_sc = load_scales("d_sc", d_scales, G)
+        load_list("k1", k1)
+        load_list("k2", k2)
+        x_sc = load_scales("x_sc", x_scales, T)
+        load_list("offs", offs)
+        load_list("hz", hz)
+        d_w = load_words("d_w", d_words, G)
+        x_w = load_words("x_w", x_words, T)
+        for name, src in (("n1", n1), ("n2", n2), ("k3", k3), ("k4", k4), ("hy", hy), ("n3", n3), ("n4", n4),
+                          ("n6", n6), ("n5", n5), ("n7", n7)):
+            load_list(name, src)
+        gs4 = keep.tile([P, PACK], F32, name="gs4")
+        nc.gpsimd.dma_start(gs4[:], gs.rearrange("(p t) o -> p (t o)", t=PACK))
+
+        planes1 = keep.tile([P, 2 * H + 2 * S], U8, name="planes1", align_bytes=64)
+        planes2 = keep.tile([P, 2 * H + S], U8, name="planes2", align_bytes=64)
+        nc.vector.memset(planes1[:].bitcast(I32), 0)
+        nc.vector.memset(planes2[:].bitcast(I32), 0)
+
+        def gather_all(dst, d_table, x_table, d_names, x_names):
+            col = 0
+            for name in d_names:
+                nc.vector.tensor_copy(dst[:, col:col + H], d_table[:].indirect(lists[name][:]))
+                col = col + H
+            for name in x_names:
+                nc.vector.tensor_copy(dst[:, col:col + S], x_table[:].indirect(lists[name][:]))
+                col = col + S
+
+        def move_rows(queue, planes, picked):
+            for r in range(4):
+                queue.dma_start(planes[r:P:32, :].bitcast(I32), picked[8 * r:P:32, :].bitcast(I32))
+
+        def deal_words(dst, src):
+            nc.vector.tensor_copy(
+                dst.bitcast(I32).rearrange("p (t c i) -> p c t i", t=PACK, i=4),
+                src.bitcast(I32).rearrange("p (c i t) -> p c t i", t=PACK, i=4),
+            )
+
+        def deal_bytes(dst, src):
+            nc.vector.tensor_copy(
+                dst.rearrange("p (a t m) -> p a t m", a=2, t=PACK),
+                src.rearrange("p (a m t) -> p a t m", a=2, t=PACK),
+            )
+
+        bytes1 = work.tile([P, 2 * H + 2 * S], U8, name="bytes1", tag="picked_bytes", align_bytes=64)
+        gather_all(bytes1, d_sc, x_sc, ("k1", "k2"), ("offs", "hz"))
+        move_rows(nc.scalar, planes1, bytes1)
+
+        dw1 = work.tile([P, 2 * H], U32, name="dw1", align_bytes=64)
+        words1 = work.tile([P, 2 * H + 2 * S], U32, name="words1", align_bytes=64)
+        for a, name in enumerate(("k1", "k2")):
+            nc.vector.tensor_copy(words1[:, a * H:(a + 1) * H], d_w[:].indirect(lists[name][:]))
+            deal_words(dw1[:, a * H:(a + 1) * H], words1[:, a * H:(a + 1) * H])
+        ds1 = work.tile([P, 2 * H], U8, name="ds1", align_bytes=64)
+        deal_bytes(ds1[:], planes1[:, 0:2 * H])
+        for a, name in enumerate(("offs", "hz")):
+            nc.vector.tensor_copy(words1[:, 2 * H + a * S:2 * H + (a + 1) * S], x_w[:].indirect(lists[name][:]))
+
+        acc1 = [psum.tile([P, S], F32, name="acc1_%d" % t) for t in range(PACK)]
+        for t in range(PACK):
+            for a in range(2):
+                mov = slice(2 * H + a * S, 2 * H + (a + 1) * S)
+                sta = slice(a * H + t * P, a * H + (t + 1) * P)
+                nc.tensor.matmul_mx(out=acc1[t][:], lhsT=dw1[:, sta].bitcast(FP8X4), lhsT_scale=ds1[:, sta],
+                                    rhs=words1[:, mov].bitcast(FP8X4), rhs_scale=planes1[:, mov],
+                                    start=(a == 0), stop=(a == 1))
+
+        h = [work.tile([P, S], F32, name="h_%d" % t) for t in range(PACK)]
+        for t in range(PACK):
+            nc.scalar.activation(h[t][:], acc1[t][:], ACT.Copy, scale=0.0625)
+        pab = work.tile([P, PACK, 2 * W], F32, name="pab", tag="pab", align_bytes=64)
+        sq = work.tile([P, PACK, 2 * W], F32, name="sq", tag="sq", align_bytes=64)
+        rb = work.tile([P, PACK, W], F32, name="rb")
+        ssum = work.tile([P, PACK, W], F32, name="ssum")
+        ra = work.tile([P, PACK, W], F32, name="ra")
+        ub = [work.tile([P, S], F32, name="ub_%d" % t) for t in range(PACK)]
+        for t in range(PACK):
+            nc.scalar.activation(pab[:, t, 0:W], h[t][:].indirect(lists["n1"][:]), ACT.Copy)
+            nc.scalar.activation(pab[:, t, W:2 * W], h[t][:].indirect(lists["n2"][:]), ACT.Copy)
+            nc.vector.tensor_tensor(sq[:, t, :], pab[:, t, :], pab[:, t, :], ALU.mult)
+            nc.vector.scalar_tensor_tensor(rb[:, t, :], pab[:, t, 0:W], -0.5, pab[:, t, W:2 * W], ALU.mult, ALU.add)
+            nc.vector.scalar_tensor_tensor(ssum[:, t, :], sq[:, t, 0:W], 0.25, sq[:, t, W:2 * W], ALU.add, ALU.add)
+        for t in range(PACK):
+            nc.scalar.activation(ub[t][:].indirect(lists["n2"][:]), rb[:, t, :], ACT.Copy)
+        nc.scalar.activation(ra[:], ssum[:], ACT.Sqrt)
+        for t in range(PACK):
+            nc.scalar.activation(ub[t][:].indirect(lists["n1"][:]), ra[:, t, :], ACT.Copy)
+
+        bytes2 = work.tile([P, 2 * H + S], U8, name="bytes2", tag="picked_bytes", align_bytes=64)
+        gather_all(bytes2, d_sc, x_sc, ("k4", "k3"), ("hy",))
+        move_rows(nc.sync, planes2, bytes2)
+        words2 = work.tile([P, 2 * H + S], U32, name="words2", tag="sq", align_bytes=64)
+        dw2 = work.tile([P, 2 * H], U32, name="dw2", align_bytes=64)
+        nc.vector.tensor_copy(words2[:, 2 * H:2 * H + S], x_w[:].indirect(lists["hy"][:]))
+        for a, name in enumerate(("k4", "k3")):
+            nc.vector.tensor_copy(words2[:, a * H:(a + 1) * H], d_w[:].indirect(lists[name][:]))
+            deal_words(dw2[:, a * H:(a + 1) * H], words2[:, a * H:(a + 1) * H])
+        ds2 = work.tile([P, 2 * H], U8, name="ds2", align_bytes=64)
+        deal_bytes(ds2[:], planes2[:, 0:2 * H])
+
+        zb = work.tile([P, S, PACK], BF16, name="zb", align_bytes=64)
+        for t in range(PACK):
+            nc.vector.tensor_scalar(zb[:, :, t], ub[t][:], gs4[:, t:t + 1], None, ALU.mult)
+        zw = work.tile([P, S], U32, name="zw", align_bytes=64)
+        zs = work.tile([P, S], U8, name="zs", align_bytes=64)
+        nc.vector.quantize_mx(out=zw[:].bitcast(FP8X4), scales=zs[:], in_=zb[:].rearrange("p j t -> p (j t)"))
+
+        acc2 = [psum.tile([P, S], F32, name="acc2_%d" % t) for t in range(PACK)]
+        moving = ((words2[:, 2 * H:2 * H + S], planes2[:, 2 * H:2 * H + S]), (zw[:], zs[:]))
+        for a in range(2):
+            for t in range(PACK):
+                sta = slice(a * H + t * P, a * H + (t + 1) * P)
+                nc.tensor.matmul_mx(out=acc2[t][:], lhsT=dw2[:, sta].bitcast(FP8X4), lhsT_scale=ds2[:, sta],
+                                    rhs=moving[a][0].bitcast(FP8X4), rhs_scale=moving[a][1],
+                                    start=(a == 0), stop=(a == 1))
+
+        h2 = [work.tile([P, S], F32, name="h2_%d" % t) for t in range(PACK)]
+        for t in range(PACK):
+            nc.vector.tensor_scalar(h2[t][:], acc2[t][:], 0.0625, None, ALU.mult)
+        pa2 = work.tile([P, PACK, W], F32, name="pa2")
+        pb2 = work.tile([P, PACK, W], F32, name="pb2")
+        ra2 = work.tile([P, PACK, W], F32, name="ra2")
+        g7 = work.tile([P, PACK, S], F32, name="g7")
+        y = work.tile([P, PACK, S], F32, name="y")
+        yb = work.tile([P, S, PACK], BF16, name="yb", align_bytes=64)
+        ub2 = [work.tile([P, S], F32, name="ub2_%d" % t) for t in range(PACK)]
+        out_rows = out_0.rearrange("(p t) j -> p t j", t=PACK)
+        for t in range(PACK):
+            nc.scalar.activation(pa2[:, t, :], h2[t][:].indirect(lists["n3"][:]), ACT.Copy)
+            nc.scalar.activation(pb2[:, t, :], h2[t][:].indirect(lists["n4"][:]), ACT.Copy)
+            nc.vector.tensor_tensor(ra2[:, t, :], pb2[:, t, :], pa2[:, t, :], ALU.subtract)
+            for half in range(2):
+                nc.scalar.activation(g7[:, t, half * W:(half + 1) * W],
+                                     h2[t][:].indirect(lists["n7"][:, half * 8:(half + 1) * 8]), ACT.Copy)
+            nc.scalar.activation(ub2[t][:].indirect(lists["n6"][:]), pa2[:, t, :], ACT.Copy)
+            nc.scalar.activation(ub2[t][:].indirect(lists["n5"][:]), ra2[:, t, :], ACT.Copy)
+            nc.vector.tensor_tensor(y[:, t, :], ub2[t][:], g7[:, t, :], ALU.max)
+            nc.sync.dma_start(out_rows[:, t, :], y[:, t, :])
+            nc.vector.tensor_copy(yb[:, :, t], y[:, t, :])
+        yw = work.tile([P, S], U32, name="yw", align_bytes=64)
+        ys = work.tile([P, S], U8, name="ys", align_bytes=64)
+        nc.vector.quantize_mx(out=yw[:].bitcast(FP8X4), scales=ys[:], in_=yb[:].rearrange("p j t -> p (j t)"))
+        nc.sync.dma_start(out_1[0].rearrange("p c r -> p (c r)").bitcast(I32), yw[:].bitcast(I32))
+        for q in range(4):
+            queue = nc.sync if q % 2 == 0 else nc.scalar
+            queue.dma_start(out_2[0][4 * q:4 * q + 4, :].bitcast(I32), ys[32 * q:32 * q + 4, :].bitcast(I32))

@@ -30,6 +30,7 @@ def tile_picked_mhhzmhpolarcphw_none_po_kernel(
     with ExitStack() as ctx:
         keep = ctx.enter_context(tc.tile_pool(name="keep", bufs=1))
         work = ctx.enter_context(tc.tile_pool(name="work", bufs=1))
+        shared = ctx.enter_context(tc.tile_pool(name="shared", bufs=1))
         psum = ctx.enter_context(tc.psum_pool(name="psum", bufs=1))
 
         lists = {}
@@ -49,12 +50,12 @@ def tile_picked_mhhzmhpolarcphw_none_po_kernel(
             nc.sync.dma_start(tile[:].bitcast(I32), src[0].rearrange("p c r -> p (c r)").bitcast(I32))
             return tile
 
-        d_sc = load_scales("d_sc", d_scales, G)
-        load_list("k1", k1)
-        load_list("k2", k2)
         x_sc = load_scales("x_sc", x_scales, T)
         load_list("offs", offs)
         load_list("hz", hz)
+        d_sc = load_scales("d_sc", d_scales, G)
+        load_list("k1", k1)
+        load_list("k2", k2)
         d_w = load_words("d_w", d_words, G)
         x_w = load_words("x_w", x_words, T)
         for name, src in (("n1", n1), ("n2", n2), ("k3", k3), ("k4", k4), ("hy", hy), ("n3", n3), ("n4", n4),
@@ -68,18 +69,20 @@ def tile_picked_mhhzmhpolarcphw_none_po_kernel(
         nc.vector.memset(planes1[:].bitcast(I32), 0)
         nc.vector.memset(planes2[:].bitcast(I32), 0)
 
-        def gather_all(dst, d_table, x_table, d_names, x_names):
-            col = 0
-            for name in d_names:
-                nc.vector.tensor_copy(dst[:, col:col + H], d_table[:].indirect(lists[name][:]))
-                col = col + H
-            for name in x_names:
-                nc.vector.tensor_copy(dst[:, col:col + S], x_table[:].indirect(lists[name][:]))
-                col = col + S
+        warm_in = keep.tile([P, 1], F32, name="warm_in")
+        warm_out = keep.tile([P, 1], F32, name="warm_out")
+        nc.vector.memset(warm_in[:], 1.0)
+        nc.scalar.activation(warm_out[:], warm_in[:], ACT.Sqrt)
 
-        def move_rows(queue, planes, picked):
+        def gather_all(dst, d_table, x_table, d_names, x_names):
+            for a, name in enumerate(x_names):
+                nc.vector.tensor_copy(dst[:, 2 * H + a * S:2 * H + (a + 1) * S], x_table[:].indirect(lists[name][:]))
+            for a, name in enumerate(d_names):
+                nc.vector.tensor_copy(dst[:, a * H:(a + 1) * H], d_table[:].indirect(lists[name][:]))
+
+        def move_rows(queue, planes, picked, src_cols, dst_cols):
             for r in range(4):
-                queue.dma_start(planes[r:P:32, :].bitcast(I32), picked[8 * r:P:32, :].bitcast(I32))
+                queue.dma_start(planes[r:P:32, dst_cols].bitcast(I32), picked[8 * r:P:32, src_cols].bitcast(I32))
 
         def deal_words(dst, src):
             nc.vector.tensor_copy(
@@ -93,32 +96,39 @@ def tile_picked_mhhzmhpolarcphw_none_po_kernel(
                 src.rearrange("p (a m t) -> p a t m", a=2, t=PACK),
             )
 
-        bytes1 = work.tile([P, 2 * H + 2 * S], U8, name="bytes1", tag="picked_bytes", align_bytes=64)
+        bytes1 = shared.tile([P, 2 * H + 2 * S], U8, name="bytes1", align_bytes=64, offset=0)
         gather_all(bytes1, d_sc, x_sc, ("k1", "k2"), ("offs", "hz"))
-        move_rows(nc.scalar, planes1, bytes1)
+        d_cols = slice(0, 2 * H)
+        move_rows(nc.scalar, planes1, bytes1, slice(0, 2 * H + 2 * S), slice(0, 2 * H + 2 * S))
 
         dw1 = work.tile([P, 2 * H], U32, name="dw1", align_bytes=64)
-        words1 = work.tile([P, 2 * H + 2 * S], U32, name="words1", align_bytes=64)
+        words1 = work.tile([P, 2 * H], U32, name="words1", align_bytes=64)
         for a, name in enumerate(("k1", "k2")):
             nc.vector.tensor_copy(words1[:, a * H:(a + 1) * H], d_w[:].indirect(lists[name][:]))
             deal_words(dw1[:, a * H:(a + 1) * H], words1[:, a * H:(a + 1) * H])
+        xw_offs = work.tile([P, S], U32, name="xw_offs", align_bytes=64)
+        nc.vector.tensor_copy(xw_offs[:], x_w[:].indirect(lists["offs"][:]))
         ds1 = work.tile([P, 2 * H], U8, name="ds1", align_bytes=64)
-        deal_bytes(ds1[:], planes1[:, 0:2 * H])
-        for a, name in enumerate(("offs", "hz")):
-            nc.vector.tensor_copy(words1[:, 2 * H + a * S:2 * H + (a + 1) * S], x_w[:].indirect(lists[name][:]))
+        deal_bytes(ds1[:], planes1[:, d_cols])
+        xw_hz = shared.tile([P, S], U32, name="xw_hz", align_bytes=64, offset=0)
+        nc.vector.tensor_copy(xw_hz[:], x_w[:].indirect(lists["hz"][:]))
+        xw1 = (xw_offs, xw_hz)
 
-        acc1 = [psum.tile([P, S], F32, name="acc1_%d" % t) for t in range(PACK)]
-        for t in range(PACK):
-            for a in range(2):
+        acc1 = [psum.tile([P, S], F32, name="acc1_%d" % t, tag="acc1_%d" % t) for t in range(PACK)]
+        for a, t in ((0, 0), (0, 1), (1, 0), (1, 1), (0, 2), (1, 2), (0, 3), (1, 3)):
+            if True:
                 mov = slice(2 * H + a * S, 2 * H + (a + 1) * S)
                 sta = slice(a * H + t * P, a * H + (t + 1) * P)
                 nc.tensor.matmul_mx(out=acc1[t][:], lhsT=dw1[:, sta].bitcast(FP8X4), lhsT_scale=ds1[:, sta],
-                                    rhs=words1[:, mov].bitcast(FP8X4), rhs_scale=planes1[:, mov],
+                                    rhs=xw1[a][:].bitcast(FP8X4), rhs_scale=planes1[:, mov],
                                     start=(a == 0), stop=(a == 1))
 
         h = [work.tile([P, S], F32, name="h_%d" % t) for t in range(PACK)]
         for t in range(PACK):
-            nc.scalar.activation(h[t][:], acc1[t][:], ACT.Copy, scale=0.0625)
+            if t < 2:
+                nc.scalar.activation(h[t][:], acc1[t][:], ACT.Copy, scale=0.0625)
+            else:
+                nc.vector.tensor_scalar(h[t][:], acc1[t][:], 0.0625, None, ALU.mult)
         pab = work.tile([P, PACK, 2 * W], F32, name="pab", tag="pab", align_bytes=64)
         sq = work.tile([P, PACK, 2 * W], F32, name="sq", tag="sq", align_bytes=64)
         rb = work.tile([P, PACK, W], F32, name="rb")
@@ -128,46 +138,63 @@ def tile_picked_mhhzmhpolarcphw_none_po_kernel(
         for t in range(PACK):
             nc.scalar.activation(pab[:, t, 0:W], h[t][:].indirect(lists["n1"][:]), ACT.Copy)
             nc.scalar.activation(pab[:, t, W:2 * W], h[t][:].indirect(lists["n2"][:]), ACT.Copy)
-            nc.vector.tensor_tensor(sq[:, t, :], pab[:, t, :], pab[:, t, :], ALU.mult)
-            nc.vector.scalar_tensor_tensor(rb[:, t, :], pab[:, t, 0:W], -0.5, pab[:, t, W:2 * W], ALU.mult, ALU.add)
-            nc.vector.scalar_tensor_tensor(ssum[:, t, :], sq[:, t, 0:W], 0.25, sq[:, t, W:2 * W], ALU.add, ALU.add)
+            if t % 2 == 1:
+                two = slice(t - 1, t + 1)
+                nc.vector.scalar_tensor_tensor(rb[:, two, :], pab[:, two, 0:W], -0.5, pab[:, two, W:2 * W],
+                                               ALU.mult, ALU.add)
+                nc.vector.tensor_tensor(sq[:, two, :], pab[:, two, :], pab[:, two, :], ALU.mult)
+                nc.vector.scalar_tensor_tensor(ssum[:, two, :], sq[:, two, 0:W], 0.25, sq[:, two, W:2 * W],
+                                               ALU.add, ALU.add)
         for t in range(PACK):
             nc.scalar.activation(ub[t][:].indirect(lists["n2"][:]), rb[:, t, :], ACT.Copy)
         nc.scalar.activation(ra[:], ssum[:], ACT.Sqrt)
         for t in range(PACK):
             nc.scalar.activation(ub[t][:].indirect(lists["n1"][:]), ra[:, t, :], ACT.Copy)
 
-        bytes2 = work.tile([P, 2 * H + S], U8, name="bytes2", tag="picked_bytes", align_bytes=64)
+        bytes2 = shared.tile([P, 2 * H + S], U8, name="bytes2", align_bytes=64, offset=4 * S)
         gather_all(bytes2, d_sc, x_sc, ("k4", "k3"), ("hy",))
-        move_rows(nc.sync, planes2, bytes2)
+        move_rows(nc.sync, planes2, bytes2, slice(2 * H, 2 * H + S), slice(2 * H, 2 * H + S))
+        ds2 = work.tile([P, 2 * H], U8, name="ds2", tag="pab", align_bytes=64)
+        deal_bytes(ds2[:], bytes2[:, d_cols])
+        move_rows(nc.sync, planes2, ds2, d_cols, d_cols)
         words2 = work.tile([P, 2 * H + S], U32, name="words2", tag="sq", align_bytes=64)
         dw2 = work.tile([P, 2 * H], U32, name="dw2", align_bytes=64)
         nc.vector.tensor_copy(words2[:, 2 * H:2 * H + S], x_w[:].indirect(lists["hy"][:]))
         for a, name in enumerate(("k4", "k3")):
             nc.vector.tensor_copy(words2[:, a * H:(a + 1) * H], d_w[:].indirect(lists[name][:]))
             deal_words(dw2[:, a * H:(a + 1) * H], words2[:, a * H:(a + 1) * H])
-        ds2 = work.tile([P, 2 * H], U8, name="ds2", align_bytes=64)
-        deal_bytes(ds2[:], planes2[:, 0:2 * H])
 
         zb = work.tile([P, S, PACK], BF16, name="zb", align_bytes=64)
-        for t in range(PACK):
+        halves = (slice(0, W), slice(W, S))
+        for t in range(PACK - 1):
             nc.vector.tensor_scalar(zb[:, :, t], ub[t][:], gs4[:, t:t + 1], None, ALU.mult)
+        for cols in halves:
+            nc.vector.tensor_scalar(zb[:, cols, PACK - 1], ub[PACK - 1][:, cols], gs4[:, PACK - 1:PACK], None, ALU.mult)
         zw = work.tile([P, S], U32, name="zw", align_bytes=64)
         zs = work.tile([P, S], U8, name="zs", align_bytes=64)
-        nc.vector.quantize_mx(out=zw[:].bitcast(FP8X4), scales=zs[:], in_=zb[:].rearrange("p j t -> p (j t)"))
+        for cols in halves:
+            nc.vector.quantize_mx(out=zw[:, cols].bitcast(FP8X4), scales=zs[:, cols],
+                                  in_=zb[:, cols, :].rearrange("p j t -> p (j t)"))
 
-        acc2 = [psum.tile([P, S], F32, name="acc2_%d" % t) for t in range(PACK)]
-        moving = ((words2[:, 2 * H:2 * H + S], planes2[:, 2 * H:2 * H + S]), (zw[:], zs[:]))
-        for a in range(2):
-            for t in range(PACK):
+        acc2_first = [psum.tile([P, W], F32, name="acc2_first_%d" % half, tag=("acc1_0", "acc2_0")[half])
+                      for half in range(2)]
+        acc2 = [None] + [psum.tile([P, S], F32, name="acc2_%d" % t) for t in range(1, PACK)]
+        pieces2 = [(0, halves[0], acc2_first[0]), (0, halves[1], acc2_first[1])]
+        pieces2 = pieces2 + [(t, slice(0, S), acc2[t]) for t in range(1, PACK)]
+        xw_hy = words2[:, 2 * H:2 * H + S]
+        xs_hy = planes2[:, 2 * H:2 * H + S]
+        for a, (mov_w, mov_s) in enumerate(((xw_hy, xs_hy), (zw[:], zs[:]))):
+            for t, cols, acc in pieces2:
                 sta = slice(a * H + t * P, a * H + (t + 1) * P)
-                nc.tensor.matmul_mx(out=acc2[t][:], lhsT=dw2[:, sta].bitcast(FP8X4), lhsT_scale=ds2[:, sta],
-                                    rhs=moving[a][0].bitcast(FP8X4), rhs_scale=moving[a][1],
+                nc.tensor.matmul_mx(out=acc[:], lhsT=dw2[:, sta].bitcast(FP8X4), lhsT_scale=planes2[:, sta],
+                                    rhs=mov_w[:, cols].bitcast(FP8X4), rhs_scale=mov_s[:, cols],
                                     start=(a == 0), stop=(a == 1))
 
-        h2 = [work.tile([P, S], F32, name="h2_%d" % t) for t in range(PACK)]
-        for t in range(PACK):
-            nc.vector.tensor_scalar(h2[t][:], acc2[t][:], 0.0625, None, ALU.mult)
+        h2 = work.tile([P, PACK * S], F32, name="h2")
+        nc.scalar.activation(h2[:, halves[0]], acc2_first[0][:], ACT.Copy, scale=0.0625)
+        nc.vector.tensor_scalar(h2[:, halves[1]], acc2_first[1][:], 0.0625, None, ALU.mult)
+        for t in range(1, PACK):
+            nc.vector.tensor_scalar(h2[:, t * S:(t + 1) * S], acc2[t][:], 0.0625, None, ALU.mult)
         pa2 = work.tile([P, PACK, W], F32, name="pa2")
         pb2 = work.tile([P, PACK, W], F32, name="pb2")
         ra2 = work.tile([P, PACK, W], F32, name="ra2")
@@ -177,21 +204,30 @@ def tile_picked_mhhzmhpolarcphw_none_po_kernel(
         ub2 = [work.tile([P, S], F32, name="ub2_%d" % t) for t in range(PACK)]
         out_rows = out_0.rearrange("(p t) j -> p t j", t=PACK)
         for t in range(PACK):
-            nc.scalar.activation(pa2[:, t, :], h2[t][:].indirect(lists["n3"][:]), ACT.Copy)
-            nc.scalar.activation(pb2[:, t, :], h2[t][:].indirect(lists["n4"][:]), ACT.Copy)
+            nc.scalar.activation(pa2[:, t, :], h2[:, t * S:(t + 1) * S].indirect(lists["n3"][:]), ACT.Copy)
+            nc.scalar.activation(pb2[:, t, :], h2[:, t * S:(t + 1) * S].indirect(lists["n4"][:]), ACT.Copy)
             nc.vector.tensor_tensor(ra2[:, t, :], pb2[:, t, :], pa2[:, t, :], ALU.subtract)
-            for half in range(2):
-                nc.scalar.activation(g7[:, t, half * W:(half + 1) * W],
-                                     h2[t][:].indirect(lists["n7"][:, half * 8:(half + 1) * 8]), ACT.Copy)
             nc.scalar.activation(ub2[t][:].indirect(lists["n6"][:]), pa2[:, t, :], ACT.Copy)
             nc.scalar.activation(ub2[t][:].indirect(lists["n5"][:]), ra2[:, t, :], ACT.Copy)
-            nc.vector.tensor_tensor(y[:, t, :], ub2[t][:], g7[:, t, :], ALU.max)
+            if t < PACK - 1:
+                nc.scalar.activation(g7[:, t, :], h2[:, t * S:(t + 2) * S].indirect(lists["n7"][:]), ACT.Copy)
+            else:
+                for half, cols in enumerate(halves):
+                    nc.scalar.activation(g7[:, t, cols],
+                                         h2[:, t * S:(t + 1) * S].indirect(lists["n7"][:, half * 8:(half + 1) * 8]),
+                                         ACT.Copy)
+            pieces = halves if t == PACK - 1 else (slice(0, S),)
+            for cols in pieces:
+                nc.vector.tensor_tensor(y[:, t, cols], ub2[t][:, cols], g7[:, t, cols], ALU.max)
             nc.sync.dma_start(out_rows[:, t, :], y[:, t, :])
-            nc.vector.tensor_copy(yb[:, :, t], y[:, t, :])
+            for cols in pieces:
+                nc.vector.tensor_copy(yb[:, cols, t], y[:, t, cols])
         yw = work.tile([P, S], U32, name="yw", align_bytes=64)
         ys = work.tile([P, S], U8, name="ys", align_bytes=64)
-        nc.vector.quantize_mx(out=yw[:].bitcast(FP8X4), scales=ys[:], in_=yb[:].rearrange("p j t -> p (j t)"))
+        for cols in halves:
+            nc.vector.quantize_mx(out=yw[:, cols].bitcast(FP8X4), scales=ys[:, cols],
+                                  in_=yb[:, cols, :].rearrange("p j t -> p (j t)"))
         nc.sync.dma_start(out_1[0].rearrange("p c r -> p (c r)").bitcast(I32), yw[:].bitcast(I32))
         for q in range(4):
-            queue = nc.sync if q % 2 == 0 else nc.scalar
+            queue = nc.sync if q == 0 else nc.scalar
             queue.dma_start(out_2[0][4 * q:4 * q + 4, :].bitcast(I32), ys[32 * q:32 * q + 4, :].bitcast(I32))

from contextlib import ExitStack

import concourse.mybir as mybir

F32 = mybir.dt.float32
BF16 = mybir.dt.bfloat16
I32 = mybir.dt.int32
U32 = mybir.dt.uint32
U16 = mybir.dt.uint16
U8 = mybir.dt.uint8
FP8X4 = mybir.dt.float8_e4m3fn_x4
ALU = mybir.AluOpType
ACT = mybir.ActivationFunctionType

P = 128
PACK = 4
T = 1024
G = 2048
S = 256
H = 512
W = 128
FLOPS = 4 * 2 * 512 * H * S


def tile_picked_mhhzmhpolarcphw_none_po_kernel(
    tc, x_words, x_scales, d_words, d_scales, gs, offs, k1, hz, k2, n1, n2, k3, k4, hy, n3, n4, n5, n6, n7,
    out_0, out_1, out_2,
):
    nc = tc.nc
    with ExitStack() as ctx:
        keep = ctx.enter_context(tc.tile_pool(name="keep", bufs=1))
        work = ctx.enter_context(tc.tile_pool(name="work", bufs=1))
        shared = ctx.enter_context(tc.tile_pool(name="shared", bufs=1))
        psum = ctx.enter_context(tc.psum_pool(name="psum", bufs=1))

        lists = {}

        def load_list(name, src):
            lists[name] = keep.tile([P, src.shape[1]], U16, name="list_" + name)
            nc.sync.dma_start(lists[name][:], src)

        def load_scales(name, src, width):
            tile = keep.tile([P, width], U8, name=name, align_bytes=64)
            rows = src[0].bitcast(I32)
            nc.sync.dma_start(tile[:].bitcast(I32), rows.unsqueeze(1).to_broadcast([16, 8, width // 4]))
            return tile

        def load_words(name, src, width):
            tile = keep.tile([P, width], U32, name=name, align_bytes=64)
            nc.sync.dma_start(tile[:].bitcast(I32), src[0].rearrange("p c r -> p (c r)").bitcast(I32))
            return tile

        x_sc = load_scales("x_sc", x_scales, T)
        load_list("offs", offs)
        load_list("hz", hz)
        d_sc = load_scales("d_sc", d_scales, G)
        load_list("k1", k1)
        load_list("k2", k2)
        d_w = load_words("d_w", d_words, G)
        x_w = load_words("x_w", x_words, T)
        for name, src in (("n1", n1), ("n2", n2), ("k3", k3), ("k4", k4), ("hy", hy), ("n3", n3), ("n4", n4),
                          ("n6", n6), ("n5", n5), ("n7", n7)):
            load_list(name, src)
        gs4 = keep.tile([P, PACK], F32, name="gs4")
        nc.gpsimd.dma_start(gs4[:], gs.rearrange("(p t) o -> p (t o)", t=PACK))

        planes1 = keep.tile([P, 2 * H + 2 * S], U8, name="planes1", align_bytes=64)
        planes2 = keep.tile([P, 2 * H + S], U8, name="planes2", align_bytes=64)
        nc.vector.memset(planes1[:].bitcast(I32), 0)
        nc.vector.memset(planes2[:].bitcast(I32), 0)

        warm_in = keep.tile([P, 1], F32, name="warm_in")
        warm_out = keep.tile([P, 1], F32, name="warm_out")
        nc.vector.memset(warm_in[:], 1.0)
        nc.scalar.activation(warm_out[:], warm_in[:], ACT.Sqrt)

        def gather_all(dst, d_table, x_table, d_names, x_names):
            for a, name in enumerate(x_names):
                nc.vector.tensor_copy(dst[:, 2 * H + a * S:2 * H + (a + 1) * S], x_table[:].indirect(lists[name][:]))
            for a, name in enumerate(d_names):
                nc.vector.tensor_copy(dst[:, a * H:(a + 1) * H], d_table[:].indirect(lists[name][:]))

        def move_rows(queue, planes, picked, src_cols, dst_cols):
            for r in range(4):
                queue.dma_start(planes[r:P:32, dst_cols].bitcast(I32), picked[8 * r:P:32, src_cols].bitcast(I32))

        def deal_words(dst, src):
            nc.vector.tensor_copy(
                dst.bitcast(I32).rearrange("p (t c i) -> p c t i", t=PACK, i=4),
                src.bitcast(I32).rearrange("p (c i t) -> p c t i", t=PACK, i=4),
            )

        def deal_bytes(dst, src):
            nc.vector.tensor_copy(
                dst.rearrange("p (a t m) -> p a t m", a=2, t=PACK),
                src.rearrange("p (a m t) -> p a t m", a=2, t=PACK),
            )

        bytes1 = shared.tile([P, 2 * H + 2 * S], U8, name="bytes1", align_bytes=64, offset=0)
        gather_all(bytes1, d_sc, x_sc, ("k1", "k2"), ("offs", "hz"))
        d_cols = slice(0, 2 * H)
        move_rows(nc.scalar, planes1, bytes1, slice(0, 2 * H + 2 * S), slice(0, 2 * H + 2 * S))

        dw1 = work.tile([P, 2 * H], U32, name="dw1", align_bytes=64)
        words1 = work.tile([P, 2 * H], U32, name="words1", align_bytes=64)
        for a, name in enumerate(("k1", "k2")):
            nc.vector.tensor_copy(words1[:, a * H:(a + 1) * H], d_w[:].indirect(lists[name][:]))
            deal_words(dw1[:, a * H:(a + 1) * H], words1[:, a * H:(a + 1) * H])
        xw_offs = work.tile([P, S], U32, name="xw_offs", align_bytes=64)
        nc.vector.tensor_copy(xw_offs[:], x_w[:].indirect(lists["offs"][:]))
        ds1 = work.tile([P, 2 * H], U8, name="ds1", align_bytes=64)
        deal_bytes(ds1[:], planes1[:, d_cols])
        xw_hz = shared.tile([P, S], U32, name="xw_hz", align_bytes=64, offset=0)
        nc.vector.tensor_copy(xw_hz[:], x_w[:].indirect(lists["hz"][:]))
        xw1 = (xw_offs, xw_hz)

        acc1 = [psum.tile([P, S], F32, name="acc1_%d" % t, tag="acc1_%d" % t) for t in range(PACK)]
        for a, t in ((0, 0), (0, 1), (1, 0), (1, 1), (0, 2), (1, 2), (0, 3), (1, 3)):
            if True:
                mov = slice(2 * H + a * S, 2 * H + (a + 1) * S)
                sta = slice(a * H + t * P, a * H + (t + 1) * P)
                nc.tensor.matmul_mx(out=acc1[t][:], lhsT=dw1[:, sta].bitcast(FP8X4), lhsT_scale=ds1[:, sta],
                                    rhs=xw1[a][:].bitcast(FP8X4), rhs_scale=planes1[:, mov],
                                    start=(a == 0), stop=(a == 1))

        h = [work.tile([P, S], F32, name="h_%d" % t) for t in range(PACK)]
        for t in range(PACK):
            if t < 2:
                nc.scalar.activation(h[t][:], acc1[t][:], ACT.Copy, scale=0.0625)
            else:
                nc.vector.tensor_scalar(h[t][:], acc1[t][:], 0.0625, None, ALU.mult)
        pab = work.tile([P, PACK, 2 * W], F32, name="pab", tag="pab", align_bytes=64)
        sq = work.tile([P, PACK, 2 * W], F32, name="sq", tag="sq", align_bytes=64)
        rb = work.tile([P, PACK, W], F32, name="rb")
        ssum = work.tile([P, PACK, W], F32, name="ssum")
        ra = work.tile([P, PACK, W], F32, name="ra")
        ub = [work.tile([P, S], F32, name="ub_%d" % t) for t in range(PACK)]
        for t in range(PACK):
            nc.scalar.activation(pab[:, t, 0:W], h[t][:].indirect(lists["n1"][:]), ACT.Copy)
            nc.scalar.activation(pab[:, t, W:2 * W], h[t][:].indirect(lists["n2"][:]), ACT.Copy)
            if t % 2 == 1:
                two = slice(t - 1, t + 1)
                nc.vector.scalar_tensor_tensor(rb[:, two, :], pab[:, two, 0:W], -0.5, pab[:, two, W:2 * W],
                                               ALU.mult, ALU.add)
                nc.vector.tensor_tensor(sq[:, two, :], pab[:, two, :], pab[:, two, :], ALU.mult)
                nc.vector.scalar_tensor_tensor(ssum[:, two, :], sq[:, two, 0:W], 0.25, sq[:, two, W:2 * W],
                                               ALU.add, ALU.add)
        for t in range(PACK):
            nc.scalar.activation(ub[t][:].indirect(lists["n2"][:]), rb[:, t, :], ACT.Copy)
        nc.scalar.activation(ra[:], ssum[:], ACT.Sqrt)
        for t in range(PACK):
            nc.scalar.activation(ub[t][:].indirect(lists["n1"][:]), ra[:, t, :], ACT.Copy)

        bytes2 = shared.tile([P, 2 * H + S], U8, name="bytes2", align_bytes=64, offset=4 * S)
        gather_all(bytes2, d_sc, x_sc, ("k4", "k3"), ("hy",))
        move_rows(nc.sync, planes2, bytes2, slice(2 * H, 2 * H + S), slice(2 * H, 2 * H + S))
        ds2 = work.tile([P, 2 * H], U8, name="ds2", tag="pab", align_bytes=64)
        deal_bytes(ds2[:], bytes2[:, d_cols])
        move_rows(nc.sync, planes2, ds2, d_cols, d_cols)
        words2 = work.tile([P, 2 * H + S], U32, name="words2", tag="sq", align_bytes=64)
        dw2 = work.tile([P, 2 * H], U32, name="dw2", align_bytes=64)
        nc.vector.tensor_copy(words2[:, 2 * H:2 * H + S], x_w[:].indirect(lists["hy"][:]))
        for a, name in enumerate(("k4", "k3")):
            nc.vector.tensor_copy(words2[:, a * H:(a + 1) * H], d_w[:].indirect(lists[name][:]))
            deal_words(dw2[:, a * H:(a + 1) * H], words2[:, a * H:(a + 1) * H])

        zb = work.tile([P, S, PACK], BF16, name="zb", align_bytes=64)
        halves = (slice(0, W), slice(W, S))
        for t in range(PACK - 1):
            nc.vector.tensor_scalar(zb[:, :, t], ub[t][:], gs4[:, t:t + 1], None, ALU.mult)
        for cols in halves:
            nc.vector.tensor_scalar(zb[:, cols, PACK - 1], ub[PACK - 1][:, cols], gs4[:, PACK - 1:PACK], None, ALU.mult)
        zw = work.tile([P, S], U32, name="zw", align_bytes=64)
        zs = work.tile([P, S], U8, name="zs", align_bytes=64)
        for cols in halves:
            nc.vector.quantize_mx(out=zw[:, cols].bitcast(FP8X4), scales=zs[:, cols],
                                  in_=zb[:, cols, :].rearrange("p j t -> p (j t)"))

        acc2_first = [psum.tile([P, W], F32, name="acc2_first_%d" % half, tag=("acc1_0", "acc2_0")[half])
                      for half in range(2)]
        acc2 = [None] + [psum.tile([P, S], F32, name="acc2_%d" % t) for t in range(1, PACK)]
        pieces2 = [(0, halves[0], acc2_first[0]), (0, halves[1], acc2_first[1])]
        pieces2 = pieces2 + [(t, slice(0, S), acc2[t]) for t in range(1, PACK)]
        xw_hy = words2[:, 2 * H:2 * H + S]
        xs_hy = planes2[:, 2 * H:2 * H + S]
        for a, (mov_w, mov_s) in enumerate(((xw_hy, xs_hy), (zw[:], zs[:]))):
            for t, cols, acc in pieces2:
                sta = slice(a * H + t * P, a * H + (t + 1) * P)
                nc.tensor.matmul_mx(out=acc[:], lhsT=dw2[:, sta].bitcast(FP8X4), lhsT_scale=planes2[:, sta],
                                    rhs=mov_w[:, cols].bitcast(FP8X4), rhs_scale=mov_s[:, cols],
                                    start=(a == 0), stop=(a == 1))

        h2 = work.tile([P, PACK * S], F32, name="h2")
        nc.scalar.activation(h2[:, halves[0]], acc2_first[0][:], ACT.Copy, scale=0.0625)
        nc.vector.tensor_scalar(h2[:, halves[1]], acc2_first[1][:], 0.0625, None, ALU.mult)
        for t in range(1, PACK):
            nc.vector.tensor_scalar(h2[:, t * S:(t + 1) * S], acc2[t][:], 0.0625, None, ALU.mult)
        pa2 = work.tile([P, PACK, W], F32, name="pa2")
        pb2 = work.tile([P, PACK, W], F32, name="pb2")
        ra2 = work.tile([P, PACK, W], F32, name="ra2")
        g7 = work.tile([P, PACK, S], F32, name="g7")
        y = work.tile([P, PACK, S], F32, name="y")
        yb = work.tile([P, S, PACK], BF16, name="yb", align_bytes=64)
        ub2 = [work.tile([P, S], F32, name="ub2_%d" % t) for t in range(PACK)]
        out_rows = out_0.rearrange("(p t) j -> p t j", t=PACK)
        for t in range(PACK):
            nc.scalar.activation(pa2[:, t, :], h2[:, t * S:(t + 1) * S].indirect(lists["n3"][:]), ACT.Copy)
            nc.scalar.activation(pb2[:, t, :], h2[:, t * S:(t + 1) * S].indirect(lists["n4"][:]), ACT.Copy)
            nc.vector.tensor_tensor(ra2[:, t, :], pb2[:, t, :], pa2[:, t, :], ALU.subtract)
            nc.scalar.activation(ub2[t][:].indirect(lists["n6"][:]), pa2[:, t, :], ACT.Copy)
            nc.scalar.activation(ub2[t][:].indirect(lists["n5"][:]), ra2[:, t, :], ACT.Copy)
            if t < PACK - 1:
                nc.scalar.activation(g7[:, t, :], h2[:, t * S:(t + 2) * S].indirect(lists["n7"][:]), ACT.Copy)
            else:
                for half, cols in enumerate(halves):
                    nc.scalar.activation(g7[:, t, cols],
                                         h2[:, t * S:(t + 1) * S].indirect(lists["n7"][:, half * 8:(half + 1) * 8]),
                                         ACT.Copy)
            pieces = halves if t == PACK - 1 else (slice(0, S),)
            for cols in pieces:
                nc.vector.tensor_tensor(y[:, t, cols], ub2[t][:, cols], g7[:, t, cols], ALU.max)
            nc.sync.dma_start(out_rows[:, t, :], y[:, t, :])
            for cols in pieces:
                nc.vector.tensor_copy(yb[:, cols, t], y[:, t, cols])
        yw = work.tile([P, S], U32, name="yw", align_bytes=64)
        ys = work.tile([P, S], U8, name="ys", align_bytes=64)
        for cols in halves:
            nc.vector.quantize_mx(out=yw[:, cols].bitcast(FP8X4), scales=ys[:, cols],
                                  in_=yb[:, cols, :].rearrange("p j t -> p (j t)"))
        nc.sync.dma_start(out_1[0].rearrange("p c r -> p (c r)").bitcast(I32), yw[:].bitcast(I32))
        for q in range(4):
            queue = nc.sync if q == 0 else nc.scalar
            queue.dma_start(out_2[0][4 * q:4 * q + 4, :].bitcast(I32), ys[32 * q:32 * q + 4, :].bitcast(I32))
